import numpy as np
import ml_dtypes


def mxq(x, axis, fmt="e4m3"):
    dtype, down = {"e4m3": (ml_dtypes.float8_e4m3fn, 7), "e5m2": (ml_dtypes.float8_e5m2, 14)}[fmt]
    v = np.moveaxis(np.asarray(x, np.float32).astype(ml_dtypes.bfloat16).astype(np.float64), axis, -1)
    blocks = v.reshape(v.shape[:-1] + (-1, 32))
    amax = np.abs(blocks).max(-1, keepdims=True)
    byte = np.maximum(np.where(amax > 0, np.frexp(amax)[1] - 1 + 127, 0) - down, 1)
    scale = np.exp2(byte - 127.0)
    codes = (blocks / scale).astype(np.float32).astype(dtype).astype(np.float64)
    return np.moveaxis((codes * scale).reshape(v.shape), -1, axis)


WIDE = False


def mx_kscale(k):
    if not WIDE:
        return np.ones(k)
    levels = np.array([10, -10, 5, -5, 0])
    if k % 512:
        return np.exp2(np.random.permutation(np.resize(levels, k // 32))).repeat(32)
    a = np.empty((k // 512, 16))
    for p in range(k // 512):
        a[p, :8] = np.random.permutation(np.resize(levels, 8))
        for g in range(8):
            far = levels[np.abs(levels - a[p, g]) >= 10]
            a[p, g + 8] = far[np.random.randint(len(far))]
    return np.exp2(a.ravel()).repeat(32)


def f64(x):
    return np.asarray(x).astype(np.float64)


def striped(idx):
    return np.tile(idx.reshape(-1, 16).T, (8, 1)).astype(np.uint16)


def unstriped(offs):
    return offs[:16].T.reshape(-1).astype(np.int64)


E2M1 = np.array([0.0, 0.5, 1.0, 1.5, 2.0, 3.0, 4.0, 6.0, -0.0, -0.5, -1.0, -1.5, -2.0, -3.0, -4.0, -6.0])


def pack_weight(w, fmt):
    k, n = w.shape
    w = f64(np.asarray(w, np.float32).astype(ml_dtypes.bfloat16)).reshape(k // 32, 32, n)
    amax = np.abs(w).max(1)
    if fmt == "e4m3":
        byte = np.frexp(amax)[1] - 1 + 127 - 7
    else:
        mant, ex = np.frexp(amax / 6.0)
        byte = np.where(mant > 0.5, ex, ex - 1) + 127
    byte = np.clip(np.where(amax > 0, byte, 1), 1, 254)
    scaled = (w * np.exp2(127.0 - byte)[:, None, :]).reshape(k, n).astype(np.float32)
    by_word = np.ascontiguousarray(scaled.reshape(k // 512, 128, 4, n).transpose(0, 1, 3, 2))
    if fmt == "e4m3":
        words = by_word.astype(ml_dtypes.float8_e4m3fn).view(np.uint8)
    else:
        c = by_word.astype(ml_dtypes.float4_e2m1fn).view(np.uint8) & 0xF
        words = (c[..., 0::2] | (c[..., 1::2] << 4)).reshape(k // 512, 128, 2 * n)
    return np.ascontiguousarray(words), np.ascontiguousarray(byte.astype(np.uint8).reshape(k // 512, 16, n))


def unpack_weight(words, scales, fmt):
    g, _, n = scales.shape
    words = np.ascontiguousarray(words).reshape(g, 128, n, -1)
    if fmt == "e4m3":
        vals = words.view(ml_dtypes.float8_e4m3fn).astype(np.float64)
    else:
        nib = np.empty((g, 128, n, 4), np.uint8)
        nib[..., 0::2] = words & 0xF
        nib[..., 1::2] = words >> 4
        vals = E2M1[nib]
    vals = vals * np.repeat(np.exp2(scales.astype(np.float64) - 127.0), 8, axis=1)[..., None]
    return vals.transpose(0, 1, 3, 2).reshape(g * 512, n)


def gelu(v):
    return 0.5 * v * (1.0 + np.tanh(np.sqrt(2.0 / np.pi) * (v + 0.044715 * v**3)))


T, K, H, S, T2, P = 2048, 1536, 1024, 512, 1024, 512

def setup_inputs():
    n = np.random.standard_normal
    s = mx_kscale(K)[:, None]
    u = mx_kscale(H)[:, None]
    d = {}
    d["tab_words"], d["tab_scales"] = pack_weight(n((K, T)) * s, "e4m3")
    d["offs"] = striped(np.random.permutation(T)[:S])
    d["w1"] = (n((K, H)) / s * u.T / K ** 0.5).astype(np.float32)
    d["w4_words"], d["w4_scales"] = pack_weight(n((K, H)) / s / K ** 0.5, "e2m1")
    d["wgs"] = np.exp(0.3 * n((128, S))).astype(np.float32)
    d["page0"] = (n((H, T2)) * u).astype(np.float32)
    d["offs2"] = striped(np.random.permutation(T2)[:S])
    d["offs3"] = striped(np.random.permutation(T2)[:P])
    d["cap"] = (np.random.uniform(-0.4, 0.8, H) * u[:, 0]).astype(np.float32)
    sign = np.sign(n(H))
    d["sens"] = (sign * np.random.uniform(0.6, 1.4, H) / u[:, 0] ** 2 / H ** 0.5).astype(np.float32)
    d["slot"] = (1.6 * np.exp(0.3 * n(T2))).astype(np.float32)
    return d

def reference(tab_words, tab_scales, offs, w1, w4_words, w4_scales, wgs, page0, offs2, offs3, cap, sens, slot):
    v = unpack_weight(tab_words, tab_scales, "e4m3")[:, unstriped(offs)]
    w4 = unpack_weight(w4_words, w4_scales, "e2m1")
    a = mxq(f64(w1), 0, "e4m3").T @ v
    b = w4.T @ v
    h = np.abs(b) * a
    page = f64(page0).copy()
    page[:, unstriped(offs2)] = np.tile(f64(wgs), (H // 128, 1)) * h
    x = np.minimum(page[:, unstriped(offs3)], f64(cap)[:, None])
    x = x * f64(sens)[:, None]
    e = mxq(page, 0, "e4m3").T @ mxq(x, 0, "e4m3")
    y = e * f64(slot)[:, None]
    return y / (1.0 + np.exp(-y))

from contextlib import ExitStack

import concourse.mybir as mybir
from concourse.masks import make_identity

T, K, H, S, T2, NX = 2048, 1536, 1024, 512, 1024, 512
FLOPS = 2 * (2 * K * H * S + H * T2 * NX)

F32 = mybir.dt.float32
BF16 = mybir.dt.bfloat16
I32 = mybir.dt.int32
U32 = mybir.dt.uint32
U16 = mybir.dt.uint16
U8 = mybir.dt.uint8
FP8X4 = mybir.dt.float8_e4m3fn_x4
FP4X4 = mybir.dt.float4_e2m1fn_x4
ALU = mybir.AluOpType
ACT = mybir.ActivationFunctionType

P = 128
PACK = 4
KP = P * PACK
A = K // KP
B = H // KP
NT = B * PACK
HALF = T2 // 2


def tile_list_escalator_step_match_kernel(
    tc, tab_words, tab_scales, offs, w1, w4_words, w4_scales, wgs, page0, offs2, offs3, cap, sens, slot, out
):
    nc = tc.nc
    with ExitStack() as ctx:
        lists = ctx.enter_context(tc.tile_pool(name="lists", bufs=1))
        sb = ctx.enter_context(tc.tile_pool(name="sb", bufs=1))
        psum = ctx.enter_context(tc.psum_pool(name="psum", bufs=1))

        def new(shape, dtype, tag, bufs=1):
            return sb.tile(shape, dtype, name=tag, tag=tag, bufs=bufs, align_bytes=64)

        def bank(n):
            return psum.tile([P, S], F32, name="bank%d" % n, tag="bank%d" % n)

        idx = lists.tile([P, S // 16], U16, name="idx")
        idx2 = lists.tile([P, S // 16], U16, name="idx2")
        idx3 = lists.tile([P, NX // 16], U16, name="idx3")

        tab_sc = new([P, A * T], U8, "tab_sc")
        w4_sc = new([P, A * H], U8, "w4_sc")
        nc.vector.memset(w4_sc[:].bitcast(I32), 0)
        nc.vector.memset(tab_sc[:].bitcast(I32), 0)
        identity = new([P, P], F32, "identity")
        make_identity(nc, identity[:])

        def load_scales(plane, rows):
            for q in range(4):
                nc.sync.dma_start(
                    out=plane[:].bitcast(I32)[32 * q : 32 * q + 4, :].rearrange("r (a w) -> r a w", a=A),
                    in_=rows[:, 4 * q : 4 * q + 4, :].bitcast(I32).rearrange("a r w -> r a w"),
                )

        wgs_raw = new([P, S], F32, "a_even")
        nc.sync.dma_start(out=wgs_raw[:], in_=wgs)
        w4_raw = new([P, A * H // 2], I32, "w4_raw")
        nc.sync.dma_start(
            out=w4_raw[:].rearrange("p (a w) -> p a w", a=A),
            in_=w4_words.bitcast(I32).rearrange("a p w -> p a w"),
        )
        load_scales(w4_sc, w4_scales)
        nc.sync.dma_start(idx[:], offs)
        load_scales(tab_sc, tab_scales)
        tab_w = []
        for a in range(A):
            tab_w.append(new([P, T], U32, "tab%d" % a))
            nc.sync.dma_start(
                out=tab_w[a][:].bitcast(I32), in_=tab_words[a].rearrange("p t i -> p (t i)").bitcast(I32)
            )

        w1_raw = {}
        pages = {}
        page_rows = page0.rearrange("(b p t) m -> b t p m", b=B, t=PACK)

        def load_w1(b, a):
            w1_raw[b, a] = new([P, PACK, KP], F32, "raw%d" % (A * b + a))
            nc.sync.dma_start(
                out=w1_raw[b, a][:],
                in_=w1[KP * a : KP * (a + 1), KP * b : KP * (b + 1)].rearrange("(p j) c -> p j c", j=PACK),
            )

        def load_page(n):
            pages[n] = new([P, T2], F32, "page%d" % n)
            nc.sync.dma_start(out=pages[n][:], in_=page_rows[n // PACK, n % PACK])

        for a in range(A):
            load_w1(0, a)
        nc.sync.dma_start(idx2[:], offs2)
        load_page(0)
        load_w1(1, 0)
        nc.sync.dma_start(idx3[:], offs3)
        cap_sb = new([P, B, PACK], F32, "cap_sb")
        sens_sb = new([P, B, PACK], F32, "sens_sb")
        nc.sync.dma_start(out=cap_sb[:], in_=cap.rearrange("(b p t) -> p b t", b=B, t=PACK))
        nc.sync.dma_start(out=sens_sb[:], in_=sens.rearrange("(b p t) -> p b t", b=B, t=PACK))
        load_page(1)
        load_w1(1, 1)
        load_w1(1, 2)
        for n in range(2, NT):
            load_page(n)
        slot_sb = new([P, T2 // P], F32, "slot_sb")
        with nc.allow_non_contiguous_dma(reason="one value a partition"):
            nc.sync.dma_start(out=slot_sb[:], in_=slot.rearrange("(c p) -> p c", p=P))

        turned = bank(7)
        for c in range(S // P):
            nc.tensor.transpose(turned[:, P * c : P * (c + 1)], wgs_raw[:, P * c : P * (c + 1)], identity[:])
        dealt = new([P, S // P, PACK, 4, 32], F32, "dealt")
        nc.scalar.copy(
            out=dealt[:],
            in_=turned[:].rearrange("j (c m t) -> j c t m", t=PACK, m=32).unsqueeze(3).to_broadcast(
                [P, S // P, PACK, 4, 32]
            ),
        )
        wgs_t = []
        for t in range(PACK):
            back = bank(5 + t % 2)
            for c in range(S // P):
                nc.tensor.transpose(
                    back[:, P * c : P * (c + 1)], dealt[:, c, t].rearrange("j g m -> j (g m)"), identity[:]
                )
            wgs_t.append(new([P, S], F32, "wgs%d" % t))
            nc.scalar.activation(out=wgs_t[t][:], in_=back[:], func=ACT.Copy)

        w4_c = new([P, A * H], U16, "w4_c")
        nc.scalar.copy(
            out=w4_c[:].rearrange("p (c t m) -> p c t m", t=PACK, m=P),
            in_=w4_raw[:].bitcast(U16).rearrange("p (c m t) -> p c t m", t=PACK, m=P),
        )
        w4_s = new([P, A * H], U8, "w4_s")
        nc.vector.tensor_copy(
            out=w4_s[:].rearrange("p (c t m) -> p c t m", t=PACK, m=P),
            in_=w4_sc[:].rearrange("p (c m t) -> p c t m", t=PACK, m=P),
        )
        v_c, v_sc = [], []
        for a in range(A):
            v_sc.append(new([P, S], U8, "v_sc%d" % a))
            nc.vector.tensor_copy(v_sc[a][:], tab_sc[:, T * a : T * (a + 1)].indirect(idx[:]))
            v_c.append(new([P, S], U32, "v_c%d" % a))
            nc.vector.tensor_copy(v_c[a][:], tab_w[a][:].indirect(idx[:]))

        b_acc = {}

        def product_b(tiles):
            for n in tiles:
                b_acc[n] = bank(n % 5)
            for a in range(A):
                for n in tiles:
                    cols = slice(H * a + P * n, H * a + P * (n + 1))
                    nc.tensor.matmul_mx(
                        out=b_acc[n][:], lhsT=w4_c[:, cols].bitcast(FP4X4), lhsT_scale=w4_s[:, cols],
                        rhs=v_c[a][:].bitcast(FP8X4), rhs_scale=v_sc[a][:], start=(a == 0), stop=(a == A - 1),
                    )

        product_b(range(5))
        bw = {}

        def weigh_b(n):
            size = new([P, S], F32, {1: "after_bw1", 2: "after_bw2"}.get(n, "size"))
            nc.scalar.activation(out=size[:], in_=b_acc[n][:], func=ACT.Abs)
            bw[n] = new([P, S], F32, "bw%d" % n)
            nc.vector.tensor_tensor(bw[n][:], size[:], wgs_t[n % PACK][:], ALU.mult)

        w1_c, w1_s, a_acc, a_sb = {}, {}, {}, {}

        def quantise_w1(b, a, t0, nt, copy, woven):
            copy(
                out=woven.rearrange("p (t m j) -> p m j t", t=nt, j=PACK),
                in_=w1_raw[b, a][:].rearrange("p j (m t) -> p m j t", t=PACK)[:, :, :, t0 : t0 + nt],
            )
            codes = new([P, nt * P], U32, "w1_c%d%d%d" % (b, a, t0))
            scales = new([P, nt * P], U8, "w1_s%d%d%d" % (b, a, t0))
            nc.vector.quantize_mx(out=codes[:].bitcast(FP8X4), scales=scales[:], in_=woven)
            for t in range(nt):
                w1_c[b, a, t0 + t] = codes[:, P * t : P * (t + 1)]
                w1_s[b, a, t0 + t] = scales[:, P * t : P * (t + 1)]

        def product_a(n):
            b, t = divmod(n, PACK)
            a_acc[n] = bank((5, 6, 7, 3, 4, 0, 1, 2)[n])
            for a in range(A):
                nc.tensor.matmul_mx(
                    out=a_acc[n][:], lhsT=w1_c[b, a, t].bitcast(FP8X4), lhsT_scale=w1_s[b, a, t],
                    rhs=v_c[a][:].bitcast(FP8X4), rhs_scale=v_sc[a][:], start=(a == 0), stop=(a == A - 1),
                )

        a_tags = ["bw5", "bw6", "bw7", "a_odd", "a_even", "a_odd", "a_even", "a_odd"]

        def fetch_a(n):
            a_sb[n] = new([P, S], F32, a_tags[n])
            (nc.vector.tensor_copy if n == 0 else nc.scalar.copy)(out=a_sb[n][:], in_=a_acc[n][:])

        x_pairs, page_pairs = {}, {}
        x_c, x_s, pg_c, pg_s = {}, {}, {}, {}

        def scatter(n):
            nc.vector.tensor_tensor(pages[n][:].indirect(idx2[:]), a_sb[n][:], bw[n][:], ALU.mult)

        def pick(n):
            b, t = divmod(n, PACK)
            picked = new([P, NX], F32, "picked", bufs=2)
            nc.vector.tensor_copy(picked[:], pages[n][:].indirect(idx3[:]))
            if t == 0:
                x_pairs[b] = new([P, 2, NX, 2], BF16, ("dealt", "x_pairs")[b])
            nc.vector.tensor_scalar(
                x_pairs[b][:, t // 2, :, t % 2], picked[:], cap_sb[:, b, t : t + 1], sens_sb[:, b, t : t + 1],
                ALU.min, ALU.mult,
            )

        pair_tags = {(0, 0): "raw4", (0, 1): "raw3", (1, 0): "raw1", (1, 1): "raw2"}
        woven_tags = {(0, 0): "tab0", (0, 1): "tab1", (1, 0): "tab2", (1, 1): "raw0"}

        def round_page(n, h):
            b, t = divmod(n, PACK)
            if t == 0:
                page_pairs[b, h] = new([P, 2, HALF, 2], BF16, pair_tags[b, h])
            nc.scalar.copy(out=page_pairs[b, h][:, t // 2, :, t % 2], in_=pages[n][:, HALF * h : HALF * (h + 1)])

        def weave_and_quantise(pairs, tag, copy, name):
            woven = new([P, PACK * HALF], BF16, tag)
            copy(
                out=woven[:].bitcast(F32).rearrange("p (m u) -> p m u", u=2),
                in_=pairs[:].rearrange("p u m e -> p (u m e)").bitcast(F32).rearrange("p (u m) -> p m u", u=2),
            )
            codes = new([P, HALF], U32, name + "_c")
            scales = new([P, HALF], U8, name + "_s")
            nc.vector.quantize_mx(out=codes[:].bitcast(FP8X4), scales=scales[:], in_=woven[:])
            return codes, scales

        def quantise_page(b, h, copy):
            pg_c[b, h], pg_s[b, h] = weave_and_quantise(page_pairs[b, h], woven_tags[b, h], copy, "pg%d%d" % (b, h))

        def quantise_x(b, copy):
            x_c[b], x_s[b] = weave_and_quantise(x_pairs[b], ("w4_raw", "tab_sc")[b], copy, "x%d" % b)

        e_acc = {}

        def product_e(c, b):
            h, cc = divmod(c, HALF // P)
            cols = slice(P * cc, P * (cc + 1))
            if b == 0:
                e_acc[c] = bank(c)
            nc.tensor.matmul_mx(
                out=e_acc[c][:], lhsT=pg_c[b, h][:, cols].bitcast(FP8X4), lhsT_scale=pg_s[b, h][:, cols],
                rhs=x_c[b][:].bitcast(FP8X4), rhs_scale=x_s[b][:], start=(b == 0), stop=(b == B - 1),
            )

        on_vector, on_scalar = nc.vector.tensor_copy, nc.scalar.copy

        def quantise_w1_half(b, t0, tag):
            woven = new([P, A * 2 * KP], BF16, tag)
            for a in range(A):
                quantise_w1(b, a, t0, 2, on_scalar, woven[:, 2 * KP * a : 2 * KP * (a + 1)])

        def replace_columns(n):
            if n >= 3:
                weigh_b(n)
            product_a(n)
            fetch_a(n)
            scatter(n)
            pick(n)

        def round_whole_page(n):
            round_page(n, 0)
            round_page(n, 1)

        quantise_w1(0, 0, 0, 2, on_vector, new([P, 2 * KP], BF16, "w1_bf")[:])
        weigh_b(0)
        weigh_b(1)
        quantise_w1(0, 1, 0, 2, on_vector, new([P, 2 * KP], BF16, "after_bw1")[:])
        weigh_b(2)
        quantise_w1(0, 2, 0, 1, on_vector, new([P, KP], BF16, "after_bw2")[:])
        quantise_w1(0, 2, 1, 1, on_vector, new([P, KP], BF16, "w1_bf")[:])
        replace_columns(0)
        replace_columns(1)
        quantise_w1_half(0, 2, "after_bw2")
        replace_columns(2)
        product_b(range(5, NT))
        quantise_w1_half(1, 0, "bw0")
        replace_columns(3)
        quantise_w1_half(1, 2, "bw1")
        replace_columns(4)
        for n in range(4):
            round_whole_page(n)
        replace_columns(5)
        quantise_page(0, 0, on_scalar)
        quantise_page(0, 1, on_scalar)
        quantise_x(0, on_scalar)
        replace_columns(6)
        round_whole_page(4)
        round_whole_page(5)
        weigh_b(7)
        product_a(7)
        fetch_a(7)
        round_whole_page(6)
        for c in range(T2 // P):
            product_e(c, 0)
        scatter(7)
        pick(7)
        round_page(7, 0)
        quantise_x(1, on_vector)
        quantise_page(1, 0, on_scalar)
        round_page(7, 1)
        quantise_page(1, 1, on_vector)
        for c in range(T2 // P):
            product_e(c, 1)
            result = new([P, NX], F32, "bw%d" % c)
            nc.scalar.activation(out=result[:], in_=e_acc[c][:], func=ACT.Silu, scale=slot_sb[:, c : c + 1])
            nc.sync.dma_start(out=out[P * c : P * (c + 1), :], in_=result[:])
